import numpy as np
import ml_dtypes


def mxq(x, axis, fmt="e4m3"):
    dtype, down = {"e4m3": (ml_dtypes.float8_e4m3fn, 7), "e5m2": (ml_dtypes.float8_e5m2, 14)}[fmt]
    v = np.moveaxis(np.asarray(x, np.float32).astype(ml_dtypes.bfloat16).astype(np.float64), axis, -1)
    blocks = v.reshape(v.shape[:-1] + (-1, 32))
    amax = np.abs(blocks).max(-1, keepdims=True)
    byte = np.maximum(np.where(amax > 0, np.frexp(amax)[1] - 1 + 127, 0) - down, 1)
    scale = np.exp2(byte - 127.0)
    codes = (blocks / scale).astype(np.float32).astype(dtype).astype(np.float64)
    return np.moveaxis((codes * scale).reshape(v.shape), -1, axis)


WIDE = False


def mx_kscale(k):
    if not WIDE:
        return np.ones(k)
    levels = np.array([10, -10, 5, -5, 0])
    if k % 512:
        return np.exp2(np.random.permutation(np.resize(levels, k // 32))).repeat(32)
    a = np.empty((k // 512, 16))
    for p in range(k // 512):
        a[p, :8] = np.random.permutation(np.resize(levels, 8))
        for g in range(8):
            far = levels[np.abs(levels - a[p, g]) >= 10]
            a[p, g + 8] = far[np.random.randint(len(far))]
    return np.exp2(a.ravel()).repeat(32)


def f64(x):
    return np.asarray(x).astype(np.float64)


def striped(idx):
    return np.tile(np.asarray(idx).reshape(-1, 16).T, (8, 1)).astype(np.uint16)


def unstriped(offs):
    return offs[:16].T.reshape(-1).astype(np.int64)


E2M1 = np.array([0.0, 0.5, 1.0, 1.5, 2.0, 3.0, 4.0, 6.0, -0.0, -0.5, -1.0, -1.5, -2.0, -3.0, -4.0, -6.0])


def pack_weight(w, fmt):
    k, n = w.shape
    w = f64(np.asarray(w, np.float32).astype(ml_dtypes.bfloat16)).reshape(k // 32, 32, n)
    amax = np.abs(w).max(1)
    if fmt == "e4m3":
        byte = np.frexp(amax)[1] - 1 + 127 - 7
    else:
        mant, ex = np.frexp(amax / 6.0)
        byte = np.where(mant > 0.5, ex, ex - 1) + 127
    byte = np.clip(np.where(amax > 0, byte, 1), 1, 254)
    scaled = (w * np.exp2(127.0 - byte)[:, None, :]).reshape(k, n).astype(np.float32)
    by_word = np.ascontiguousarray(scaled.reshape(k // 512, 128, 4, n).transpose(0, 1, 3, 2))
    if fmt == "e4m3":
        words = by_word.astype(ml_dtypes.float8_e4m3fn).view(np.uint8)
    else:
        c = by_word.astype(ml_dtypes.float4_e2m1fn).view(np.uint8) & 0xF
        words = (c[..., 0::2] | (c[..., 1::2] << 4)).reshape(k // 512, 128, 2 * n)
    return np.ascontiguousarray(words), np.ascontiguousarray(byte.astype(np.uint8).reshape(k // 512, 16, n))


def unpack_weight(words, scales, fmt):
    g, _, n = scales.shape
    words = np.ascontiguousarray(words).reshape(g, 128, n, -1)
    if fmt == "e4m3":
        vals = words.view(ml_dtypes.float8_e4m3fn).astype(np.float64)
    else:
        nib = np.empty((g, 128, n, 4), np.uint8)
        nib[..., 0::2] = words & 0xF
        nib[..., 1::2] = words >> 4
        vals = E2M1[nib]
    vals = vals * np.repeat(np.exp2(scales.astype(np.float64) - 127.0), 8, axis=1)[..., None]
    return vals.transpose(0, 1, 3, 2).reshape(g * 512, n)


K, R, F, T, J, G = 512, 128, 512, 2048, 512, 32


def setup_inputs():
    n = np.random.standard_normal
    idx = np.random.permutation(T)[:J]
    fk = mx_kscale(K)
    ff = mx_kscale(F)
    tabp = pack_weight(n((K, T)) / fk[:, None], "e2m1")
    dtabp = pack_weight(n((K, T)) / fk[:, None], "e2m1")
    return {
        "tab_words": tabp[0],
        "tab_scales": tabp[1],
        "w1": (n((K, R)) * 1 / np.sqrt(K) * fk[:, None]).astype(np.float32),
        "sharp": (np.random.uniform(0.3, 1.5, (R, 1))).astype(np.float32),
        "wo": (n((F, R)) * 1 / np.sqrt(F) * ff[:, None]).astype(np.float32),
        "dy": (n((F, J)) / ff[:, None]).astype(np.float32),
        "dtab_words": dtabp[0],
        "dtab_scales": dtabp[1],
        "og": (np.random.uniform(0.7, 2.0, (R, 1))).astype(np.float32),
        "base": (0.3 * n((R, J))).astype(np.float32),
        "offs": striped(idx),
    }


def reference(tab_words, tab_scales, w1, sharp, wo, dy, dtab_words, dtab_scales, og, base, offs):
    idx = unstriped(offs)
    tabu = unpack_weight(tab_words, tab_scales, "e2m1")
    dtabu = unpack_weight(dtab_words, dtab_scales, "e2m1")
    w1q = mxq(f64(w1), 0, "e4m3")
    tabidxg = tabu[:, idx]
    a = w1q.T @ tabidxg
    dtabidxg = dtabu[:, idx]
    ta = w1q.T @ dtabidxg
    m1 = a.reshape(R, G, J // G).mean(axis=2)
    mr = np.repeat(m1, J // G, axis=1)
    ce = a - mr
    woq = mxq(f64(wo), 0, "e4m3")
    dyq = mxq(f64(dy), 0, "e4m3")
    c0 = woq.T @ dyq
    xm1 = ta.reshape(R, G, J // G).mean(axis=2)
    xmr = np.repeat(xm1, J // G, axis=1)
    xce = ta - xmr
    xdce = ((ta * c0 - xce * ce * 2.0 * f64(sharp) * (np.square(ce) * f64(sharp) + 1.0) * 2.0 * c0 * a / np.square(np.square(ce) * f64(sharp) + 1.0)) / np.square(np.square(ce) * f64(sharp) + 1.0) * (-1.0) * f64(sharp) * ce + xce * c0 * a / np.square(np.square(ce) * f64(sharp) + 1.0) * (-1.0) * f64(sharp)) * 2.0
    xdmr = xdce * (-1.0)
    xdm1 = xdmr.reshape(R, G, J // G).sum(axis=2)
    xe1 = xdm1 / 16.0
    xr1 = np.repeat(xe1, J // G, axis=1)
    xda = xce * ce * 2.0 * f64(sharp) * c0 / np.square(np.square(ce) * f64(sharp) + 1.0) * (-1.0) + xdce + xr1
    y = xda * f64(og) + f64(base)
    return y

@@ -1,0 +1,187 @@
+from contextlib import ExitStack
+
+import concourse.mybir as mybir
+
+K, R, F, T, J, G = 512, 128, 512, 2048, 512, 32
+GROUP = J // G
+FLOPS = 3 * 2 * K * R * J
+
+F32 = mybir.dt.float32
+BF16 = mybir.dt.bfloat16
+I32 = mybir.dt.int32
+U32 = mybir.dt.uint32
+U16 = mybir.dt.uint16
+U8 = mybir.dt.uint8
+FP8X4 = mybir.dt.float8_e4m3fn_x4
+FP4X4 = mybir.dt.float4_e2m1fn_x4
+ALU = mybir.AluOpType
+ACT = mybir.ActivationFunctionType
+AXIS = mybir.AxisListType
+
+P = 128
+PACK = 4
+PARTS = 2
+WIDTH = J // PARTS
+DY_PARTS = 2
+
+
+def tile_attend_hvcontrastpool_kernel(tc, tab_words, tab_scales, w1, sharp, wo, dy, dtab_words, dtab_scales, og, base, offs, out):
+    nc = tc.nc
+    with ExitStack() as ctx:
+        pool = ctx.enter_context(tc.tile_pool(name="held", bufs=1))
+        psum = ctx.enter_context(tc.psum_pool(name="psum", bufs=1))
+
+        def sb(name, shape, dtype):
+            return pool.tile(shape, dtype, name=name, align_bytes=64)
+
+        offsets = sb("offsets", [P, J // 16], U16)
+        nc.sync.dma_start(offsets[:], offs)
+
+        def load_words(name, words):
+            tile = sb(name, [P, T], U16)
+            nc.sync.dma_start(tile[:].bitcast(I32), words[0].bitcast(I32))
+            return tile
+
+        def zeroed_plane(name):
+            tile = sb(name, [P, T], U8)
+            nc.vector.memset(tile[:].bitcast(I32), 0)
+            return tile
+
+        def load_scales(tile, scales):
+            for quad in range(4):
+                nc.sync.dma_start(tile[32 * quad : 32 * quad + 4, :].bitcast(I32), scales[0, 4 * quad : 4 * quad + 4, :].bitcast(I32))
+
+        def load_rows(name, rows):
+            tile = sb(name, [P, PACK, rows.shape[1]], F32)
+            nc.sync.dma_start(tile[:], rows.rearrange("(p t) w -> p t w", t=PACK))
+            return tile
+
+        def load_plain(name, src):
+            tile = sb(name, list(src.shape), F32)
+            nc.sync.dma_start(tile[:], src)
+            return tile
+
+        tab_plane = zeroed_plane("tab_plane")
+        dtab_plane = zeroed_plane("dtab_plane")
+        tab_win = load_words("tab_win", tab_words)
+        w1_raw = load_rows("w1_raw", w1)
+        load_scales(tab_plane, tab_scales)
+        dtab_win = load_words("dtab_win", dtab_words)
+        sharp_col = load_plain("sharp_col", sharp)
+        dy_width = J // DY_PARTS
+        dy_raw = [load_rows("dy_raw%d" % i, dy[:, i * dy_width : (i + 1) * dy_width]) for i in range(DY_PARTS)]
+        load_scales(dtab_plane, dtab_scales)
+        wo_raw = load_rows("wo_raw", wo)
+        og_col = load_plain("og_col", og)
+        base_sb = load_plain("base_sb", base)
+
+        def interleave(dst, raw):
+            nc.scalar.copy(dst.rearrange("p (c i t) -> p c t i", i=4, t=PACK), raw[:].rearrange("p t (c i) -> p c t i", i=4))
+
+        def quantise(name, grouped, width):
+            codes = sb(name + "_codes", [P, width], U32)
+            scales = sb(name + "_scales", [P, width], U8)
+            nc.vector.quantize_mx(out=codes[:].bitcast(FP8X4), scales=scales[:], in_=grouped)
+            return codes, scales
+
+        def gather(name, window, dtype):
+            tile = sb(name, [P, J], dtype)
+            nc.vector.tensor_copy(tile[:], window[:].indirect(offsets[:]))
+            return tile
+
+        def product(name, stat, codes, scales):
+            bank = psum.tile([P, J], F32, name=name)
+            nc.tensor.matmul_mx(out=bank[:], lhsT=stat[0][:].bitcast(FP8X4), lhsT_scale=stat[1][:], rhs=codes, rhs_scale=scales, start=True, stop=True)
+            return bank
+
+        def cols(h):
+            return slice(h * WIDTH, (h + 1) * WIDTH)
+
+        def parts(name, width=WIDTH):
+            return [sb("%s%d" % (name, h), [P, width], F32) for h in range(PARTS)]
+
+        def grouped_view(ap):
+            return ap.rearrange("p (g i) -> p g i", i=GROUP)
+
+        def centre(name, source, addend):
+            sums = parts(name + "_sums", WIDTH // GROUP)
+            result = parts(name)
+            for h in range(PARTS):
+                nc.vector.tensor_reduce(sums[h][:], grouped_view(source[h]), AXIS.X, ALU.add)
+            for h in range(PARTS):
+                spread = sums[h][:].unsqueeze(2).to_broadcast([P, WIDTH // GROUP, GROUP])
+                nc.vector.scalar_tensor_tensor(grouped_view(result[h][:]), spread, -1.0 / GROUP, grouped_view(addend[h]), ALU.mult, ALU.add)
+            return result
+
+        w1_bf = sb("w1_bf", [P, PACK * R], BF16)
+        interleave(w1_bf[:], w1_raw)
+        tab_codes = gather("tab_codes", tab_win, U16)
+        tab_bytes = gather("tab_bytes", tab_plane, U8)
+        w1_q = quantise("w1", w1_bf[:], R)
+        a_bank = product("a_bank", w1_q, tab_codes[:].bitcast(FP4X4), tab_bytes[:])
+        a = [a_bank[:, cols(h)] for h in range(PARTS)]
+        dtab_codes = gather("dtab_codes", dtab_win, U16)
+        ce = centre("ce", a, a)
+
+        ce_sq, d_sq, d_4th, u, u_sq = parts("ce_sq"), parts("d_sq"), parts("d_4th"), parts("u"), parts("u_sq")
+        for h in range(PARTS):
+            nc.scalar.activation(ce_sq[h][:], ce[h][:], ACT.Square)
+        for h in range(PARTS):
+            nc.scalar.activation(d_sq[h][:], ce_sq[h][:], ACT.Square, bias=1.0, scale=sharp_col[:])
+        for h in range(PARTS):
+            nc.scalar.activation(u[h][:], d_sq[h][:], ACT.Abs_reciprocal_sqrt)
+        for h in range(PARTS):
+            nc.scalar.activation(d_4th[h][:], d_sq[h][:], ACT.Square)
+        for h in range(PARTS):
+            nc.scalar.activation(u_sq[h][:], d_4th[h][:], ACT.Abs_reciprocal_sqrt)
+
+        dtab_bytes = gather("dtab_bytes", dtab_plane, U8)
+        ta_bank = product("ta_bank", w1_q, dtab_codes[:].bitcast(FP4X4), dtab_bytes[:])
+        ta = [ta_bank[:, cols(h)] for h in range(PARTS)]
+
+        dy_bf = sb("dy_bf", [P, PACK * J], BF16)
+        for i in range(DY_PARTS):
+            interleave(dy_bf[:, i * PACK * dy_width : (i + 1) * PACK * dy_width], dy_raw[i])
+        wo_bf = sb("wo_bf", [P, PACK * R], BF16)
+        interleave(wo_bf[:], wo_raw)
+        gain = sb("gain", [P, 1], F32)
+        nc.gpsimd.tensor_scalar(gain[:], sharp_col[:], og_col[:], -2.0, ALU.mult, ALU.mult)
+
+        xce = centre("xce", ta, ta)
+        wo_q = quantise("wo", wo_bf[:], R)
+        dy_q = quantise("dy", dy_bf[:], J)
+        c_bank = product("c_bank", wo_q, dy_q[0][:].bitcast(FP8X4), dy_q[1][:])
+
+        def mul(name, x, y):
+            res = parts(name)
+            for h in range(PARTS):
+                nc.vector.tensor_tensor(res[h][:], x[h], y[h], ALU.mult)
+            return [t[:] for t in res]
+
+        def add(name, x, y):
+            res = parts(name)
+            for h in range(PARTS):
+                nc.vector.tensor_tensor(res[h][:], x[h], y[h], ALU.add)
+            return [t[:] for t in res]
+
+        def fused(name, x, scalar, y, op0, op1):
+            res = parts(name)
+            for h in range(PARTS):
+                nc.vector.scalar_tensor_tensor(res[h][:], x[h], scalar, y[h], op0, op1)
+            return [t[:] for t in res]
+
+        ce_v = [t[:] for t in ce]
+        xce_v = [t[:] for t in xce]
+        ce_ta = mul("ce_ta", ce_v, ta)
+        ce_xce = mul("ce_xce", ce_v, xce_v)
+        bend = fused("bend", [t[:] for t in u], -0.75, a, ALU.add, ALU.mult)
+        bend_xce = mul("bend_xce", bend, xce_v)
+        inner = fused("inner", bend_xce, 4.0, ce_ta, ALU.mult, ALU.add)
+        weight = fused("weight", [c_bank[:, cols(h)] for h in range(PARTS)], gain[:], [t[:] for t in u_sq], ALU.mult, ALU.mult)
+        xdce = mul("xdce", weight, inner)
+        direct = mul("direct", weight, ce_xce)
+        with_base = add("with_base", direct, [base_sb[:, cols(h)] for h in range(PARTS)])
+        total = add("total", with_base, xdce)
+        result = centre("result", xdce, total)
+        for h in range(PARTS):
+            nc.sync.dma_start(out[:, cols(h)], result[h][:])

@@ -1,6 +1,7 @@
 from contextlib import ExitStack
 
 import concourse.mybir as mybir
+from concourse.masks import make_identity
 
 K, R, F, T, J, G = 512, 128, 512, 2048, 512, 32
 GROUP = J // G
@@ -31,52 +32,57 @@ def tile_attend_hvcontrastpool_kernel(tc, tab_words, tab_scales, w1, sharp, wo, 
         pool = ctx.enter_context(tc.tile_pool(name="held", bufs=1))
         psum = ctx.enter_context(tc.psum_pool(name="psum", bufs=1))
 
-        def sb(name, shape, dtype):
-            return pool.tile(shape, dtype, name=name, align_bytes=64)
+        def sb(name, shape, dtype, tag=None):
+            return pool.tile(shape, dtype, name=name, tag=tag or name, align_bytes=64)
+
+        warm_in = sb("warm_in", [P, 1], F32)
+        warm_out = sb("warm_out", [P, 1], F32)
+        nc.gpsimd.memset(warm_in[:], 1.0)
+        nc.scalar.activation(warm_out[:], warm_in[:], ACT.Abs_reciprocal_sqrt)
 
         offsets = sb("offsets", [P, J // 16], U16)
         nc.sync.dma_start(offsets[:], offs)
 
-        def load_words(name, words):
-            tile = sb(name, [P, T], U16)
+        def load_words(name, words, tag=None):
+            tile = sb(name, [P, T], U16, tag=tag)
             nc.sync.dma_start(tile[:].bitcast(I32), words[0].bitcast(I32))
             return tile
 
-        def zeroed_plane(name):
-            tile = sb(name, [P, T], U8)
-            nc.vector.memset(tile[:].bitcast(I32), 0)
-            return tile
-
-        def load_scales(tile, scales):
+        def load_scales(queue, tile, scales):
             for quad in range(4):
-                nc.sync.dma_start(tile[32 * quad : 32 * quad + 4, :].bitcast(I32), scales[0, 4 * quad : 4 * quad + 4, :].bitcast(I32))
+                queue.dma_start(tile[32 * quad : 32 * quad + 4, :].bitcast(I32), scales[0, 4 * quad : 4 * quad + 4, :].bitcast(I32))
 
-        def load_rows(name, rows):
-            tile = sb(name, [P, PACK, rows.shape[1]], F32)
-            nc.sync.dma_start(tile[:], rows.rearrange("(p t) w -> p t w", t=PACK))
-            return tile
+        def load_rows(dst, rows):
+            nc.sync.dma_start(dst.rearrange("p (t w) -> p t w", t=PACK), rows.rearrange("(p t) w -> p t w", t=PACK))
 
-        def load_plain(name, src):
-            tile = sb(name, list(src.shape), F32)
-            nc.sync.dma_start(tile[:], src)
-            return tile
-
-        tab_plane = zeroed_plane("tab_plane")
-        dtab_plane = zeroed_plane("dtab_plane")
+        tab_plane = sb("tab_plane", [P, T], U8)
+        dtab_plane = sb("dtab_plane", [P, T], U8)
+        nc.vector.memset(tab_plane[:, : T // 2].bitcast(I32), 0)
+        nc.gpsimd.memset(tab_plane[:, T // 2 :].bitcast(I32), 0)
+        nc.vector.memset(dtab_plane[:].bitcast(I32), 0)
+        identity = sb("identity", [P, P], F32)
+        make_identity(nc, identity[:])
         tab_win = load_words("tab_win", tab_words)
-        w1_raw = load_rows("w1_raw", w1)
-        load_scales(tab_plane, tab_scales)
+        load_scales(nc.sync, tab_plane, tab_scales)
+        w1_raw = sb("w1_raw", [P, PACK * R], F32)
+        load_rows(w1_raw[:], w1)
+        wo_raw = sb("wo_raw", [P, PACK * R], F32)
+        load_rows(wo_raw[:], wo)
         dtab_win = load_words("dtab_win", dtab_words)
-        sharp_col = load_plain("sharp_col", sharp)
         dy_width = J // DY_PARTS
-        dy_raw = [load_rows("dy_raw%d" % i, dy[:, i * dy_width : (i + 1) * dy_width]) for i in range(DY_PARTS)]
-        load_scales(dtab_plane, dtab_scales)
-        wo_raw = load_rows("wo_raw", wo)
-        og_col = load_plain("og_col", og)
-        base_sb = load_plain("base_sb", base)
+        dy_raw = [sb("dy_raw%d" % i, [P, PACK * dy_width], F32)[:] for i in range(DY_PARTS)]
+        base_sb = sb("base_sb", [P, J], F32)[:]
+        sharp_col = sb("sharp_col", [P, 1], F32)[:]
+        og_col = sb("og_col", [P, 1], F32)[:]
+        load_rows(dy_raw[0], dy[:, :dy_width])
+        load_scales(nc.sync, dtab_plane, dtab_scales)
+        load_rows(dy_raw[1], dy[:, dy_width:])
+        nc.sync.dma_start(sharp_col, sharp)
+        nc.sync.dma_start(og_col, og)
+        nc.sync.dma_start(base_sb, base)
 
         def interleave(dst, raw):
-            nc.scalar.copy(dst.rearrange("p (c i t) -> p c t i", i=4, t=PACK), raw[:].rearrange("p t (c i) -> p c t i", i=4))
+            nc.scalar.copy(dst.rearrange("p (c i t) -> p c t i", i=4, t=PACK), raw.rearrange("p (t c i) -> p c t i", t=PACK, i=4))
 
         def quantise(name, grouped, width):
             codes = sb(name + "_codes", [P, width], U32)
@@ -84,104 +90,114 @@ def tile_attend_hvcontrastpool_kernel(tc, tab_words, tab_scales, w1, sharp, wo, 
             nc.vector.quantize_mx(out=codes[:].bitcast(FP8X4), scales=scales[:], in_=grouped)
             return codes, scales
 
-        def gather(name, window, dtype):
-            tile = sb(name, [P, J], dtype)
+        def gather(name, window, dtype, tag=None):
+            tile = sb(name, [P, J], dtype, tag=tag)
             nc.vector.tensor_copy(tile[:], window[:].indirect(offsets[:]))
             return tile
 
         def product(name, stat, codes, scales):
             bank = psum.tile([P, J], F32, name=name)
-            nc.tensor.matmul_mx(out=bank[:], lhsT=stat[0][:].bitcast(FP8X4), lhsT_scale=stat[1][:], rhs=codes, rhs_scale=scales, start=True, stop=True)
+            nc.tensor.matmul_mx(out=bank[:], lhsT=stat[0].bitcast(FP8X4), lhsT_scale=stat[1], rhs=codes, rhs_scale=scales, start=True, stop=True)
             return bank
 
-        def cols(h):
-            return slice(h * WIDTH, (h + 1) * WIDTH)
-
-        def parts(name, width=WIDTH):
-            return [sb("%s%d" % (name, h), [P, width], F32) for h in range(PARTS)]
+        def cols(h, count=PARTS):
+            return slice(h * J // count, (h + 1) * J // count)
 
         def grouped_view(ap):
             return ap.rearrange("p (g i) -> p g i", i=GROUP)
 
-        def centre(name, source, addend):
-            sums = parts(name + "_sums", WIDTH // GROUP)
-            result = parts(name)
-            for h in range(PARTS):
-                nc.vector.tensor_reduce(sums[h][:], grouped_view(source[h]), AXIS.X, ALU.add)
-            for h in range(PARTS):
-                spread = sums[h][:].unsqueeze(2).to_broadcast([P, WIDTH // GROUP, GROUP])
-                nc.vector.scalar_tensor_tensor(grouped_view(result[h][:]), spread, -1.0 / GROUP, grouped_view(addend[h]), ALU.mult, ALU.add)
+        def group_sums(name, source, count, tag=None):
+            sums = []
+            for h in range(count):
+                part = sb("%s_sums%d" % (name, h), [P, G // count], F32, tag=tag)
+                nc.vector.tensor_reduce(part[:], grouped_view(source[:, cols(h, count)]), AXIS.X, ALU.add)
+                sums.append(part)
+            return sums
+
+        def less_mean(name, source, sums):
+            count = len(sums)
+            result = sb(name, [P, J], F32)[:]
+            for h in range(count):
+                spread = sums[h][:].unsqueeze(2).to_broadcast([P, G // count, GROUP])
+                nc.vector.scalar_tensor_tensor(grouped_view(result[:, cols(h, count)]), spread, -1.0 / GROUP, grouped_view(source[:, cols(h, count)]), ALU.mult, ALU.add)
             return result
 
-        w1_bf = sb("w1_bf", [P, PACK * R], BF16)
-        interleave(w1_bf[:], w1_raw)
-        tab_codes = gather("tab_codes", tab_win, U16)
-        tab_bytes = gather("tab_bytes", tab_plane, U8)
-        w1_q = quantise("w1", w1_bf[:], R)
-        a_bank = product("a_bank", w1_q, tab_codes[:].bitcast(FP4X4), tab_bytes[:])
-        a = [a_bank[:, cols(h)] for h in range(PARTS)]
-        dtab_codes = gather("dtab_codes", dtab_win, U16)
-        ce = centre("ce", a, a)
-
-        ce_sq, d_sq, d_4th, u, u_sq = parts("ce_sq"), parts("d_sq"), parts("d_4th"), parts("u"), parts("u_sq")
-        for h in range(PARTS):
-            nc.scalar.activation(ce_sq[h][:], ce[h][:], ACT.Square)
-        for h in range(PARTS):
-            nc.scalar.activation(d_sq[h][:], ce_sq[h][:], ACT.Square, bias=1.0, scale=sharp_col[:])
-        for h in range(PARTS):
-            nc.scalar.activation(u[h][:], d_sq[h][:], ACT.Abs_reciprocal_sqrt)
-        for h in range(PARTS):
-            nc.scalar.activation(d_4th[h][:], d_sq[h][:], ACT.Square)
-        for h in range(PARTS):
-            nc.scalar.activation(u_sq[h][:], d_4th[h][:], ACT.Abs_reciprocal_sqrt)
-
-        dtab_bytes = gather("dtab_bytes", dtab_plane, U8)
-        ta_bank = product("ta_bank", w1_q, dtab_codes[:].bitcast(FP4X4), dtab_bytes[:])
-        ta = [ta_bank[:, cols(h)] for h in range(PARTS)]
-
+        w_bf = sb("w_bf", [P, 2 * PACK * R], BF16)
+        interleave(w_bf[:, : PACK * R], w1_raw[:])
+        interleave(w_bf[:, PACK * R :], wo_raw[:])
         dy_bf = sb("dy_bf", [P, PACK * J], BF16)
         for i in range(DY_PARTS):
             interleave(dy_bf[:, i * PACK * dy_width : (i + 1) * PACK * dy_width], dy_raw[i])
-        wo_bf = sb("wo_bf", [P, PACK * R], BF16)
-        interleave(wo_bf[:], wo_raw)
-        gain = sb("gain", [P, 1], F32)
-        nc.gpsimd.tensor_scalar(gain[:], sharp_col[:], og_col[:], -2.0, ALU.mult, ALU.mult)
+        tab_codes = gather("tab_codes", tab_win, U16)
+        tab_bytes = gather("tab_bytes", tab_plane, U8)
+        w_codes, w_scales = quantise("w", w_bf[:], 2 * R)
+        w1_q = (w_codes[:, :R], w_scales[:, :R])
+        wo_q = (w_codes[:, R:], w_scales[:, R:])
+        a_bank = product("a_bank", w1_q, tab_codes[:].bitcast(FP4X4), tab_bytes[:])
+        a = a_bank[:]
+        dtab_codes = gather("dtab_codes", dtab_win, U16)
+        ce = less_mean("ce", a, group_sums("ce", a, PARTS))
 
-        xce = centre("xce", ta, ta)
-        wo_q = quantise("wo", wo_bf[:], R)
+        ce_sq = dy_raw[1][:, :J]
+        d_sq, d_4th, u, u_sq = [sb(name, [P, J], F32)[:] for name in ("d_sq", "d_4th", "u", "u_sq")]
+        for h in range(PARTS):
+            nc.scalar.activation(ce_sq[:, cols(h)], ce[:, cols(h)], ACT.Square)
+        nc.scalar.activation(d_sq, ce_sq, ACT.Square, bias=1.0, scale=sharp_col)
+        nc.scalar.activation(u, d_sq, ACT.Abs_reciprocal_sqrt)
+        nc.scalar.activation(d_4th, d_sq, ACT.Square)
+        nc.scalar.activation(u_sq, d_4th, ACT.Abs_reciprocal_sqrt)
+
+        dtab_bytes = gather("dtab_bytes", dtab_plane, U8)
+        ta_bank = product("ta_bank", w1_q, dtab_codes[:].bitcast(FP4X4), dtab_bytes[:])
+        ta = ta_bank[:]
+
+        gain = sb("gain", [P, 1], F32)
+        nc.gpsimd.tensor_scalar(gain[:], sharp_col, og_col, -2.0, ALU.mult, ALU.mult)
+
         dy_q = quantise("dy", dy_bf[:], J)
         c_bank = product("c_bank", wo_q, dy_q[0][:].bitcast(FP8X4), dy_q[1][:])
+        def combine(name, x, y, op, count, tag=None):
+            res = sb(name, [P, J], F32, tag=tag)[:]
+            for h in range(count):
+                nc.vector.tensor_tensor(res[:, cols(h, count)], x[:, cols(h, count)], y[:, cols(h, count)], op)
+            return res
 
-        def mul(name, x, y):
-            res = parts(name)
+        def fused(name, x, scalar, y, op0, op1, count):
+            res = sb(name, [P, J], F32)[:]
+            for h in range(count):
+                nc.vector.scalar_tensor_tensor(res[:, cols(h, count)], x[:, cols(h, count)], scalar, y[:, cols(h, count)], op0, op1)
+            return res
+
+        def summed(name, x, y, banks):
+            res = []
             for h in range(PARTS):
-                nc.vector.tensor_tensor(res[h][:], x[h], y[h], ALU.mult)
-            return [t[:] for t in res]
+                back = psum.tile([P, WIDTH], F32, name="%s_back%d" % (name, h), tag=banks[h])
+                for b in range(0, WIDTH, P):
+                    at = h * WIDTH + b
+                    turned = psum.tile([P, P], F32, name="%s_turned%d" % (name, at), tag="turned%d" % at)
+                    nc.tensor.matmul(turned[:], x[:, at : at + P], identity[:], start=True, stop=False, is_transpose=True)
+                    nc.tensor.matmul(turned[:], y[:, at : at + P], identity[:], start=False, stop=True, is_transpose=True)
+                    staged = sb("%s_staged%d" % (name, at), [P, P], F32)
+                    nc.scalar.copy(staged[:], turned[:])
+                    nc.tensor.transpose(back[:, b : b + P], staged[:], identity[:])
+                res.append(back[:])
+            return res
 
-        def add(name, x, y):
-            res = parts(name)
-            for h in range(PARTS):
-                nc.vector.tensor_tensor(res[h][:], x[h], y[h], ALU.add)
-            return [t[:] for t in res]
-
-        def fused(name, x, scalar, y, op0, op1):
-            res = parts(name)
-            for h in range(PARTS):
-                nc.vector.scalar_tensor_tensor(res[h][:], x[h], scalar, y[h], op0, op1)
-            return [t[:] for t in res]
-
-        ce_v = [t[:] for t in ce]
-        xce_v = [t[:] for t in xce]
-        ce_ta = mul("ce_ta", ce_v, ta)
-        ce_xce = mul("ce_xce", ce_v, xce_v)
-        bend = fused("bend", [t[:] for t in u], -0.75, a, ALU.add, ALU.mult)
-        bend_xce = mul("bend_xce", bend, xce_v)
-        inner = fused("inner", bend_xce, 4.0, ce_ta, ALU.mult, ALU.add)
-        weight = fused("weight", [c_bank[:, cols(h)] for h in range(PARTS)], gain[:], [t[:] for t in u_sq], ALU.mult, ALU.mult)
-        xdce = mul("xdce", weight, inner)
-        direct = mul("direct", weight, ce_xce)
-        with_base = add("with_base", direct, [base_sb[:, cols(h)] for h in range(PARTS)])
-        total = add("total", with_base, xdce)
-        result = centre("result", xdce, total)
+        ta_sums = group_sums("xce", ta, 1, tag="dy_bf")
+        ce_ta = combine("ce_ta", ce, ta, ALU.mult, 1)
+        xce = less_mean("xce", ta, ta_sums)
+        bend = fused("bend", u, -0.75, a, ALU.add, ALU.mult, PARTS)
+        bend_xce = fused("bend_xce", bend, 4.0, xce, ALU.mult, ALU.mult, PARTS)
+        inner = summed("inner", ce_ta, bend_xce, ("ta_bank", "a_bank"))
+        weight = fused("weight", c_bank[:], gain[:], u_sq, ALU.mult, ALU.mult, 1)
+        ce_xce = combine("ce_xce", ce, xce, ALU.mult, PARTS, tag="bend")
+        direct = combine("direct", weight, ce_xce, ALU.mult, PARTS)
+        with_base = summed("with_base", base_sb, direct, ("spare_bank", "c_bank"))
+        xdce = sb("xdce", [P, J], F32)[:]
         for h in range(PARTS):
-            nc.sync.dma_start(out[:, cols(h)], result[h][:])
+            nc.vector.tensor_tensor(xdce[:, cols(h)], weight[:, cols(h)], inner[h], ALU.mult)
+        centred = less_mean("centred", xdce, group_sums("centred", xdce, PARTS))
+        result = sb("result", [P, J], F32)[:]
+        for h in range(PARTS):
+            nc.vector.tensor_tensor(result[:, cols(h)], centred[:, cols(h)], with_base[h], ALU.add)
+            nc.sync.dma_start(out[:, cols(h)], result[:, cols(h)])

@@ -40,9 +40,6 @@ def tile_attend_hvcontrastpool_kernel(tc, tab_words, tab_scales, w1, sharp, wo, 
         nc.gpsimd.memset(warm_in[:], 1.0)
         nc.scalar.activation(warm_out[:], warm_in[:], ACT.Abs_reciprocal_sqrt)
 
-        offsets = sb("offsets", [P, J // 16], U16)
-        nc.sync.dma_start(offsets[:], offs)
-
         def load_words(name, words, tag=None):
             tile = sb(name, [P, T], U16, tag=tag)
             nc.sync.dma_start(tile[:].bitcast(I32), words[0].bitcast(I32))
@@ -63,6 +60,8 @@ def tile_attend_hvcontrastpool_kernel(tc, tab_words, tab_scales, w1, sharp, wo, 
         identity = sb("identity", [P, P], F32)
         make_identity(nc, identity[:])
         tab_win = load_words("tab_win", tab_words)
+        offsets = sb("offsets", [P, J // 16], U16)
+        nc.sync.dma_start(offsets[:], offs)
         load_scales(nc.sync, tab_plane, tab_scales)
         w1_raw = sb("w1_raw", [P, PACK * R], F32)
         load_rows(w1_raw[:], w1)
@@ -142,8 +141,10 @@ def tile_attend_hvcontrastpool_kernel(tc, tab_words, tab_scales, w1, sharp, wo, 
         d_sq, d_4th, u, u_sq = [sb(name, [P, J], F32)[:] for name in ("d_sq", "d_4th", "u", "u_sq")]
         for h in range(PARTS):
             nc.scalar.activation(ce_sq[:, cols(h)], ce[:, cols(h)], ACT.Square)
-        nc.scalar.activation(d_sq, ce_sq, ACT.Square, bias=1.0, scale=sharp_col)
-        nc.scalar.activation(u, d_sq, ACT.Abs_reciprocal_sqrt)
+        for h in range(PARTS):
+            nc.scalar.activation(d_sq[:, cols(h)], ce_sq[:, cols(h)], ACT.Square, bias=1.0, scale=sharp_col)
+        for h in range(PARTS):
+            nc.scalar.activation(u[:, cols(h)], d_sq[:, cols(h)], ACT.Abs_reciprocal_sqrt)
         nc.scalar.activation(d_4th, d_sq, ACT.Square)
         nc.scalar.activation(u_sq, d_4th, ACT.Abs_reciprocal_sqrt)
 

from contextlib import ExitStack

import concourse.mybir as mybir
from concourse.masks import make_identity

K, R, F, T, J, G = 512, 128, 512, 2048, 512, 32
GROUP = J // G
FLOPS = 3 * 2 * K * R * J

F32 = mybir.dt.float32
BF16 = mybir.dt.bfloat16
I32 = mybir.dt.int32
U32 = mybir.dt.uint32
U16 = mybir.dt.uint16
U8 = mybir.dt.uint8
FP8X4 = mybir.dt.float8_e4m3fn_x4
FP4X4 = mybir.dt.float4_e2m1fn_x4
ALU = mybir.AluOpType
ACT = mybir.ActivationFunctionType
AXIS = mybir.AxisListType

P = 128
PACK = 4
PARTS = 2
WIDTH = J // PARTS
DY_PARTS = 2


def tile_attend_hvcontrastpool_kernel(tc, tab_words, tab_scales, w1, sharp, wo, dy, dtab_words, dtab_scales, og, base, offs, out):
    nc = tc.nc
    with ExitStack() as ctx:
        pool = ctx.enter_context(tc.tile_pool(name="held", bufs=1))
        psum = ctx.enter_context(tc.psum_pool(name="psum", bufs=1))

        def sb(name, shape, dtype, tag=None):
            return pool.tile(shape, dtype, name=name, tag=tag or name, align_bytes=64)

        warm_in = sb("warm_in", [P, 1], F32)
        warm_out = sb("warm_out", [P, 1], F32)
        nc.gpsimd.memset(warm_in[:], 1.0)
        nc.scalar.activation(warm_out[:], warm_in[:], ACT.Abs_reciprocal_sqrt)

        def load_words(name, words, tag=None):
            tile = sb(name, [P, T], U16, tag=tag)
            nc.sync.dma_start(tile[:].bitcast(I32), words[0].bitcast(I32))
            return tile

        def load_scales(queue, tile, scales):
            for quad in range(4):
                queue.dma_start(tile[32 * quad : 32 * quad + 4, :].bitcast(I32), scales[0, 4 * quad : 4 * quad + 4, :].bitcast(I32))

        def load_rows(dst, rows):
            nc.sync.dma_start(dst.rearrange("p (t w) -> p t w", t=PACK), rows.rearrange("(p t) w -> p t w", t=PACK))

        tab_plane = sb("tab_plane", [P, T], U8)
        dtab_plane = sb("dtab_plane", [P, T], U8)
        nc.vector.memset(tab_plane[:, : T // 2].bitcast(I32), 0)
        nc.gpsimd.memset(tab_plane[:, T // 2 :].bitcast(I32), 0)
        nc.vector.memset(dtab_plane[:].bitcast(I32), 0)
        identity = sb("identity", [P, P], F32)
        make_identity(nc, identity[:])
        tab_win = load_words("tab_win", tab_words)
        offsets = sb("offsets", [P, J // 16], U16)
        nc.sync.dma_start(offsets[:], offs)
        load_scales(nc.sync, tab_plane, tab_scales)
        w1_raw = sb("w1_raw", [P, PACK * R], F32)
        load_rows(w1_raw[:], w1)
        wo_raw = sb("wo_raw", [P, PACK * R], F32)
        load_rows(wo_raw[:], wo)
        dtab_win = load_words("dtab_win", dtab_words)
        dy_width = J // DY_PARTS
        dy_raw = [sb("dy_raw%d" % i, [P, PACK * dy_width], F32)[:] for i in range(DY_PARTS)]
        base_sb = sb("base_sb", [P, J], F32)[:]
        sharp_col = sb("sharp_col", [P, 1], F32)[:]
        og_col = sb("og_col", [P, 1], F32)[:]
        load_rows(dy_raw[0], dy[:, :dy_width])
        load_scales(nc.sync, dtab_plane, dtab_scales)
        load_rows(dy_raw[1], dy[:, dy_width:])
        nc.sync.dma_start(sharp_col, sharp)
        nc.sync.dma_start(og_col, og)
        nc.sync.dma_start(base_sb, base)

        def interleave(dst, raw):
            nc.scalar.copy(dst.rearrange("p (c i t) -> p c t i", i=4, t=PACK), raw.rearrange("p (t c i) -> p c t i", t=PACK, i=4))

        def quantise(name, grouped, width):
            codes = sb(name + "_codes", [P, width], U32)
            scales = sb(name + "_scales", [P, width], U8)
            nc.vector.quantize_mx(out=codes[:].bitcast(FP8X4), scales=scales[:], in_=grouped)
            return codes, scales

        def gather(name, window, dtype, tag=None):
            tile = sb(name, [P, J], dtype, tag=tag)
            nc.vector.tensor_copy(tile[:], window[:].indirect(offsets[:]))
            return tile

        def product(name, stat, codes, scales):
            bank = psum.tile([P, J], F32, name=name)
            nc.tensor.matmul_mx(out=bank[:], lhsT=stat[0].bitcast(FP8X4), lhsT_scale=stat[1], rhs=codes, rhs_scale=scales, start=True, stop=True)
            return bank

        def cols(h, count=PARTS):
            return slice(h * J // count, (h + 1) * J // count)

        def grouped_view(ap):
            return ap.rearrange("p (g i) -> p g i", i=GROUP)

        def group_sums(name, source, count, tag=None):
            sums = []
            for h in range(count):
                part = sb("%s_sums%d" % (name, h), [P, G // count], F32, tag=tag)
                nc.vector.tensor_reduce(part[:], grouped_view(source[:, cols(h, count)]), AXIS.X, ALU.add)
                sums.append(part)
            return sums

        def less_mean(name, source, sums):
            count = len(sums)
            result = sb(name, [P, J], F32)[:]
            for h in range(count):
                spread = sums[h][:].unsqueeze(2).to_broadcast([P, G // count, GROUP])
                nc.vector.scalar_tensor_tensor(grouped_view(result[:, cols(h, count)]), spread, -1.0 / GROUP, grouped_view(source[:, cols(h, count)]), ALU.mult, ALU.add)
            return result

        w_bf = sb("w_bf", [P, 2 * PACK * R], BF16)
        interleave(w_bf[:, : PACK * R], w1_raw[:])
        interleave(w_bf[:, PACK * R :], wo_raw[:])
        dy_bf = sb("dy_bf", [P, PACK * J], BF16)
        for i in range(DY_PARTS):
            interleave(dy_bf[:, i * PACK * dy_width : (i + 1) * PACK * dy_width], dy_raw[i])
        tab_codes = gather("tab_codes", tab_win, U16)
        tab_bytes = gather("tab_bytes", tab_plane, U8)
        w_codes, w_scales = quantise("w", w_bf[:], 2 * R)
        w1_q = (w_codes[:, :R], w_scales[:, :R])
        wo_q = (w_codes[:, R:], w_scales[:, R:])
        a_bank = product("a_bank", w1_q, tab_codes[:].bitcast(FP4X4), tab_bytes[:])
        a = a_bank[:]
        dtab_codes = gather("dtab_codes", dtab_win, U16)
        ce = less_mean("ce", a, group_sums("ce", a, PARTS))

        ce_sq = dy_raw[1][:, :J]
        d_sq, d_4th, u, u_sq = [sb(name, [P, J], F32)[:] for name in ("d_sq", "d_4th", "u", "u_sq")]
        for h in range(PARTS):
            nc.scalar.activation(ce_sq[:, cols(h)], ce[:, cols(h)], ACT.Square)
        for h in range(PARTS):
            nc.scalar.activation(d_sq[:, cols(h)], ce_sq[:, cols(h)], ACT.Square, bias=1.0, scale=sharp_col)
        for h in range(PARTS):
            nc.scalar.activation(u[:, cols(h)], d_sq[:, cols(h)], ACT.Abs_reciprocal_sqrt)
        nc.scalar.activation(d_4th, d_sq, ACT.Square)
        nc.scalar.activation(u_sq, d_4th, ACT.Abs_reciprocal_sqrt)

        dtab_bytes = gather("dtab_bytes", dtab_plane, U8)
        ta_bank = product("ta_bank", w1_q, dtab_codes[:].bitcast(FP4X4), dtab_bytes[:])
        ta = ta_bank[:]

        gain = sb("gain", [P, 1], F32)
        nc.gpsimd.tensor_scalar(gain[:], sharp_col, og_col, -2.0, ALU.mult, ALU.mult)

        dy_q = quantise("dy", dy_bf[:], J)
        c_bank = product("c_bank", wo_q, dy_q[0][:].bitcast(FP8X4), dy_q[1][:])
        def combine(name, x, y, op, count, tag=None):
            res = sb(name, [P, J], F32, tag=tag)[:]
            for h in range(count):
                nc.vector.tensor_tensor(res[:, cols(h, count)], x[:, cols(h, count)], y[:, cols(h, count)], op)
            return res

        def fused(name, x, scalar, y, op0, op1, count):
            res = sb(name, [P, J], F32)[:]
            for h in range(count):
                nc.vector.scalar_tensor_tensor(res[:, cols(h, count)], x[:, cols(h, count)], scalar, y[:, cols(h, count)], op0, op1)
            return res

        def summed(name, x, y, banks):
            res = []
            for h in range(PARTS):
                back = psum.tile([P, WIDTH], F32, name="%s_back%d" % (name, h), tag=banks[h])
                for b in range(0, WIDTH, P):
                    at = h * WIDTH + b
                    turned = psum.tile([P, P], F32, name="%s_turned%d" % (name, at), tag="turned%d" % at)
                    nc.tensor.matmul(turned[:], x[:, at : at + P], identity[:], start=True, stop=False, is_transpose=True)
                    nc.tensor.matmul(turned[:], y[:, at : at + P], identity[:], start=False, stop=True, is_transpose=True)
                    staged = sb("%s_staged%d" % (name, at), [P, P], F32)
                    nc.scalar.copy(staged[:], turned[:])
                    nc.tensor.transpose(back[:, b : b + P], staged[:], identity[:])
                res.append(back[:])
            return res

        ta_sums = group_sums("xce", ta, 1, tag="dy_bf")
        ce_ta = combine("ce_ta", ce, ta, ALU.mult, 1)
        xce = less_mean("xce", ta, ta_sums)
        bend = fused("bend", u, -0.75, a, ALU.add, ALU.mult, PARTS)
        bend_xce = fused("bend_xce", bend, 4.0, xce, ALU.mult, ALU.mult, PARTS)
        inner = summed("inner", ce_ta, bend_xce, ("ta_bank", "a_bank"))
        weight = fused("weight", c_bank[:], gain[:], u_sq, ALU.mult, ALU.mult, 1)
        ce_xce = combine("ce_xce", ce, xce, ALU.mult, PARTS, tag="bend")
        direct = combine("direct", weight, ce_xce, ALU.mult, PARTS)
        with_base = summed("with_base", base_sb, direct, ("spare_bank", "c_bank"))
        xdce = sb("xdce", [P, J], F32)[:]
        for h in range(PARTS):
            nc.vector.tensor_tensor(xdce[:, cols(h)], weight[:, cols(h)], inner[h], ALU.mult)
        centred = less_mean("centred", xdce, group_sums("centred", xdce, PARTS))
        result = sb("result", [P, J], F32)[:]
        for h in range(PARTS):
            nc.vector.tensor_tensor(result[:, cols(h)], centred[:, cols(h)], with_base[h], ALU.add)
            nc.sync.dma_start(out[:, cols(h)], result[:, cols(h)])
